import numpy as np
import ml_dtypes


def mxq(x, axis, fmt="e4m3"):
    dtype, down = {"e4m3": (ml_dtypes.float8_e4m3fn, 7), "e5m2": (ml_dtypes.float8_e5m2, 14)}[fmt]
    v = np.moveaxis(np.asarray(x, np.float32).astype(ml_dtypes.bfloat16).astype(np.float64), axis, -1)
    blocks = v.reshape(v.shape[:-1] + (-1, 32))
    amax = np.abs(blocks).max(-1, keepdims=True)
    byte = np.maximum(np.where(amax > 0, np.frexp(amax)[1] - 1 + 127, 0) - down, 1)
    scale = np.exp2(byte - 127.0)
    codes = (blocks / scale).astype(np.float32).astype(dtype).astype(np.float64)
    return np.moveaxis((codes * scale).reshape(v.shape), -1, axis)


WIDE = False


def mx_kscale(k, group=512):
    if not WIDE:
        return np.ones(k)
    levels = np.array([10, -10, 5, -5, 0])
    if group != 512:
        return np.exp2(np.random.permutation(np.resize(levels, k // group))).repeat(group)
    if k % 512:
        return np.exp2(np.random.permutation(np.resize(levels, k // 32))).repeat(32)
    a = np.empty((k // 512, 16))
    for p in range(k // 512):
        a[p, :8] = np.random.permutation(np.resize(levels, 8))
        for g in range(8):
            far = levels[np.abs(levels - a[p, g]) >= 10]
            a[p, g + 8] = far[np.random.randint(len(far))]
    return np.exp2(a.ravel()).repeat(32)


def f64(x):
    return np.asarray(x).astype(np.float64)


G, D, M, N = 4, 256, 256, 512


def setup_inputs():
    n = np.random.standard_normal
    s = mx_kscale(D, 0)[:, None]
    return {
        "x": (n((G, D, N)) * s).astype(np.float32),
        "w": (n((G, D, M)) / np.sqrt(D) / s).astype(np.float32),
        "r": n((G, M, N)).astype(np.float32),
    }


def reference(x, w, r):
    xq = mxq(f64(x), 1, "e4m3")
    y = mxq(f64(w), 1, "e4m3").transpose(0, 2, 1) @ xq
    y = np.tanh(y)
    y = y + f64(r)
    return y

@@ -1,0 +1,130 @@
+from contextlib import ExitStack
+
+import concourse.mybir as mybir
+
+G, D, M, N = 4, 256, 256, 512
+FLOPS = 2 * G * D * M * N
+
+F32 = mybir.dt.float32
+BF16 = mybir.dt.bfloat16
+U32 = mybir.dt.uint32
+U8 = mybir.dt.uint8
+FP8X4 = mybir.dt.float8_e4m3fn_x4
+TANH = mybir.ActivationFunctionType.Tanh
+ADD = mybir.AluOpType.add
+
+P = 128
+PACK = 4
+ROWS = D // PACK
+SIDE = P // ROWS
+PAIRS = G // SIDE
+HALVES = M // P
+RUN = 4
+VECTOR_COLUMNS = 344
+
+
+def tile_rows_glin_tanh_res_kernel(tc, x, w, r, out):
+    nc = tc.nc
+
+    with ExitStack() as ctx:
+        sbuf = ctx.enter_context(tc.tile_pool(name="sbuf", bufs=1))
+        psum = ctx.enter_context(tc.psum_pool(name="psum", bufs=1))
+        ctx.enter_context(tc.manual_schedule())
+
+        x_raw = [sbuf.tile([P, PACK, N], F32, name="x_raw%d" % s, align_bytes=64) for s in range(PAIRS)]
+        w_raw = [sbuf.tile([P, PACK, M], F32, name="w_raw%d" % s, align_bytes=64) for s in range(PAIRS)]
+        res = [sbuf.tile([P, HALVES, N], F32, name="res%d" % g, align_bytes=64) for g in range(G)]
+        act = [sbuf.tile([P, HALVES, N], F32, name="act%d" % g, align_bytes=64) for g in range(G)]
+        x_bf = [sbuf.tile([P, N, PACK], BF16, name="x_bf%d" % s, align_bytes=64) for s in range(PAIRS)]
+        w_bf = [sbuf.tile([P, HALVES, P, PACK], BF16, name="w_bf%d" % s, align_bytes=64) for s in range(PAIRS)]
+        x_codes = [sbuf.tile([P, N], U32, name="x_codes%d" % s, align_bytes=64) for s in range(PAIRS)]
+        x_scales = [sbuf.tile([P, N], U8, name="x_scales%d" % s, align_bytes=64) for s in range(PAIRS)]
+        w_codes = [sbuf.tile([P, M], U32, name="w_codes%d" % s, align_bytes=64) for s in range(PAIRS)]
+        w_scales = [sbuf.tile([P, M], U8, name="w_scales%d" % s, align_bytes=64) for s in range(PAIRS)]
+        sums = [[psum.tile([P, N], F32, name="sums%d_%d" % (g, t)) for t in range(HALVES)] for g in range(G)]
+        warm_in = sbuf.tile([P, 1], F32, name="warm_in")
+        warm_out = sbuf.tile([P, 1], F32, name="warm_out")
+
+        for s in range(PAIRS):
+            nc.sync.dma_start(
+                out=x_raw[s][:],
+                in_=x[SIDE * s : SIDE * (s + 1)].rearrange("c (p j) n -> (c p) j n", j=PACK),
+            )
+        for s in range(PAIRS):
+            nc.sync.dma_start(
+                out=w_raw[s][:],
+                in_=w[SIDE * s : SIDE * (s + 1)].rearrange("c (p j) m -> (c p) j m", j=PACK),
+            )
+        for g in range(G):
+            nc.sync.dma_start(out=res[g][:], in_=r[g].rearrange("(p t) n -> p t n", t=HALVES))
+
+        nc.vector.memset(warm_in[:], 0.0)
+        nc.scalar.activation(out=warm_out[:], in_=warm_in[:], func=TANH)
+
+        def x_views(s, lo, hi):
+            dst = x_bf[s][:, lo:hi, :].rearrange("p (a i) j -> p a j i", i=RUN)
+            src = x_raw[s][:, :, lo:hi].rearrange("p j (a i) -> p a j i", i=RUN)
+            return dst, src
+
+        def w_views(s, t):
+            dst = w_bf[s][:, t, :, :]
+            src = w_raw[s][:].rearrange("p j (q t) -> p t q j", t=HALVES)[:, t, :, :]
+            return dst, src
+
+        def quantize_x(s):
+            nc.vector.quantize_mx(
+                out=x_codes[s][:].bitcast(FP8X4),
+                scales=x_scales[s][:],
+                in_=x_bf[s][:].rearrange("p n j -> p (n j)"),
+            )
+
+        def quantize_w(s):
+            nc.vector.quantize_mx(
+                out=w_codes[s][:].bitcast(FP8X4),
+                scales=w_scales[s][:],
+                in_=w_bf[s][:].rearrange("p t q j -> p (t q j)"),
+            )
+
+        def multiply(s):
+            for t in range(HALVES):
+                cols = slice(P * t, P * (t + 1))
+                for c in range(SIDE):
+                    rows = slice(ROWS * c, ROWS * (c + 1))
+                    nc.tensor.matmul_mx(
+                        out=sums[SIDE * s + c][t][:],
+                        lhsT=w_codes[s][rows, cols].bitcast(FP8X4),
+                        lhsT_scale=w_scales[s][rows, cols],
+                        rhs=x_codes[s][rows, :].bitcast(FP8X4),
+                        rhs_scale=x_scales[s][rows, :],
+                        start=True,
+                        stop=True,
+                    )
+
+        dst, src = x_views(0, 0, N)
+        nc.vector.tensor_copy(out=dst, in_=src)
+        quantize_x(0)
+
+        dst, src = x_views(1, 0, VECTOR_COLUMNS)
+        nc.vector.tensor_copy(out=dst, in_=src)
+        dst, src = x_views(1, VECTOR_COLUMNS, N)
+        nc.scalar.copy(out=dst, in_=src)
+        quantize_x(1)
+
+        dst, src = w_views(0, 0)
+        nc.vector.tensor_copy(out=dst, in_=src)
+        dst, src = w_views(0, 1)
+        nc.scalar.copy(out=dst, in_=src)
+        quantize_w(0)
+        multiply(0)
+
+        for t in range(HALVES):
+            dst, src = w_views(1, t)
+            nc.vector.tensor_copy(out=dst, in_=src)
+        quantize_w(1)
+        multiply(1)
+
+        for g in range(G):
+            for t in range(HALVES):
+                nc.scalar.activation(out=act[g][:, t, :], in_=sums[g][t][:], func=TANH)
+                nc.vector.tensor_tensor(out=act[g][:, t, :], in0=act[g][:, t, :], in1=res[g][:, t, :], op=ADD)
+            nc.sync.dma_start(out=out[g].rearrange("(p t) n -> p t n", t=HALVES), in_=act[g][:])

@@ -45,18 +45,28 @@ def tile_rows_glin_tanh_res_kernel(tc, x, w, r, out):
         warm_in = sbuf.tile([P, 1], F32, name="warm_in")
         warm_out = sbuf.tile([P, 1], F32, name="warm_out")
 
-        for s in range(PAIRS):
-            nc.sync.dma_start(
-                out=x_raw[s][:],
-                in_=x[SIDE * s : SIDE * (s + 1)].rearrange("c (p j) n -> (c p) j n", j=PACK),
+        def load_x(s, lo, hi, eng):
+            eng.dma_start(
+                out=x_raw[s][:, :, lo:hi],
+                in_=x[SIDE * s : SIDE * (s + 1), :, lo:hi].rearrange("c (p j) n -> (c p) j n", j=PACK),
             )
-        for s in range(PAIRS):
-            nc.sync.dma_start(
+
+        def load_w(s, eng):
+            eng.dma_start(
                 out=w_raw[s][:],
                 in_=w[SIDE * s : SIDE * (s + 1)].rearrange("c (p j) m -> (c p) j m", j=PACK),
             )
+
+        def load_r(g, eng):
+            eng.dma_start(out=res[g][:], in_=r[g].rearrange("(p t) n -> p t n", t=HALVES))
+
+        load_x(0, 0, N, nc.sync)
+        load_w(0, nc.sync)
+        load_x(1, 0, 256, nc.sync)
+        load_w(1, nc.sync)
+        load_x(1, 256, N, nc.sync)
         for g in range(G):
-            nc.sync.dma_start(out=res[g][:], in_=r[g].rearrange("(p t) n -> p t n", t=HALVES))
+            load_r(g, nc.sync)
 
         nc.vector.memset(warm_in[:], 0.0)
         nc.scalar.activation(out=warm_out[:], in_=warm_in[:], func=TANH)
@@ -71,25 +81,25 @@ def tile_rows_glin_tanh_res_kernel(tc, x, w, r, out):
             src = w_raw[s][:].rearrange("p j (q t) -> p t q j", t=HALVES)[:, t, :, :]
             return dst, src
 
-        def quantize_x(s):
+        def quantize_x(s, lo, hi):
             nc.vector.quantize_mx(
-                out=x_codes[s][:].bitcast(FP8X4),
-                scales=x_scales[s][:],
-                in_=x_bf[s][:].rearrange("p n j -> p (n j)"),
+                out=x_codes[s][:, lo:hi].bitcast(FP8X4),
+                scales=x_scales[s][:, lo:hi],
+                in_=x_bf[s][:, lo:hi, :].rearrange("p n j -> p (n j)"),
             )
 
-        def quantize_w(s):
+        def quantize_w(s, lo, hi):
             nc.vector.quantize_mx(
-                out=w_codes[s][:].bitcast(FP8X4),
-                scales=w_scales[s][:],
-                in_=w_bf[s][:].rearrange("p t q j -> p (t q j)"),
+                out=w_codes[s][:, P * lo : P * hi].bitcast(FP8X4),
+                scales=w_scales[s][:, P * lo : P * hi],
+                in_=w_bf[s][:, lo:hi, :, :].rearrange("p t q j -> p (t q j)"),
             )
 
         def multiply(s):
-            for t in range(HALVES):
-                cols = slice(P * t, P * (t + 1))
-                for c in range(SIDE):
-                    rows = slice(ROWS * c, ROWS * (c + 1))
+            for c in range(SIDE):
+                rows = slice(ROWS * c, ROWS * (c + 1))
+                for t in range(HALVES):
+                    cols = slice(P * t, P * (t + 1))
                     nc.tensor.matmul_mx(
                         out=sums[SIDE * s + c][t][:],
                         lhsT=w_codes[s][rows, cols].bitcast(FP8X4),
@@ -100,31 +110,59 @@ def tile_rows_glin_tanh_res_kernel(tc, x, w, r, out):
                         stop=True,
                     )
 
-        dst, src = x_views(0, 0, N)
-        nc.vector.tensor_copy(out=dst, in_=src)
-        quantize_x(0)
-
-        dst, src = x_views(1, 0, VECTOR_COLUMNS)
-        nc.vector.tensor_copy(out=dst, in_=src)
-        dst, src = x_views(1, VECTOR_COLUMNS, N)
-        nc.scalar.copy(out=dst, in_=src)
-        quantize_x(1)
-
-        dst, src = w_views(0, 0)
-        nc.vector.tensor_copy(out=dst, in_=src)
-        dst, src = w_views(0, 1)
-        nc.scalar.copy(out=dst, in_=src)
-        quantize_w(0)
-        multiply(0)
-
-        for t in range(HALVES):
-            dst, src = w_views(1, t)
+        def vx(s, lo, hi):
+            dst, src = x_views(s, lo, hi)
             nc.vector.tensor_copy(out=dst, in_=src)
-        quantize_w(1)
-        multiply(1)
 
+        def sx(s, lo, hi):
+            dst, src = x_views(s, lo, hi)
+            nc.scalar.copy(out=dst, in_=src)
+
+        def vw(s, t):
+            dst, src = w_views(s, t)
+            nc.vector.tensor_copy(out=dst, in_=src)
+
+        def sw(s, t):
+            dst, src = w_views(s, t)
+            nc.scalar.copy(out=dst, in_=src)
+
+        def vw_all(s):
+            nc.vector.tensor_copy(out=w_bf[s][:], in_=w_raw[s][:].rearrange("p j (q t) -> p t q j", t=HALVES))
+
+        def tanh(g, t):
+            nc.scalar.activation(out=act[g][:, t, :], in_=sums[g][t][:], func=TANH)
+
+        def add(g, t):
+            nc.vector.tensor_tensor(out=act[g][:, t, :], in0=act[g][:, t, :], in1=res[g][:, t, :], op=ADD)
+
+        def store(g, eng):
+            eng.dma_start(out=out[g].rearrange("(p t) n -> p t n", t=HALVES), in_=act[g][:])
+
+        sx(0, 344, N)
+        vx(0, 0, 256)
+        vx(0, 256, 344)
+        quantize_x(0, 0, 256)
+        quantize_x(0, 256, N)
+        sw(0, 0)
+        vw(0, 1)
+        quantize_w(0, 0, 1)
+        quantize_w(0, 1, 2)
+        multiply(0)
+        vx(1, 0, 256)
+        tanh(0, 0)
+        tanh(0, 1)
+        vw_all(1)
+        quantize_x(1, 0, 256)
+        quantize_w(1, 0, 2)
+        sx(1, 424, N)
+        vx(1, 256, 424)
+        quantize_x(1, 256, N)
+        multiply(1)
+        tanh(1, 0)
+        tanh(1, 1)
         for g in range(G):
             for t in range(HALVES):
-                nc.scalar.activation(out=act[g][:, t, :], in_=sums[g][t][:], func=TANH)
-                nc.vector.tensor_tensor(out=act[g][:, t, :], in0=act[g][:, t, :], in1=res[g][:, t, :], op=ADD)
-            nc.sync.dma_start(out=out[g].rearrange("(p t) n -> p t n", t=HALVES), in_=act[g][:])
+                if g >= SIDE:
+                    tanh(g, t)
+                add(g, t)
+            store(g, nc.sync)

@@ -62,9 +62,8 @@ def tile_rows_glin_tanh_res_kernel(tc, x, w, r, out):
 
         load_x(0, 0, N, nc.sync)
         load_w(0, nc.sync)
-        load_x(1, 0, 256, nc.sync)
+        load_x(1, 0, N, nc.sync)
         load_w(1, nc.sync)
-        load_x(1, 256, N, nc.sync)
         for g in range(G):
             load_r(g, nc.sync)
 
@@ -138,31 +137,42 @@ def tile_rows_glin_tanh_res_kernel(tc, x, w, r, out):
         def store(g, eng):
             eng.dma_start(out=out[g].rearrange("(p t) n -> p t n", t=HALVES), in_=act[g][:])
 
-        sx(0, 344, N)
+        def vwq(s, lo, hi):
+            nc.vector.tensor_copy(
+                out=w_bf[s][:, :, lo:hi, :].rearrange("p t (a b) j -> p a j b t", b=2),
+                in_=w_raw[s][:, :, HALVES * lo : HALVES * hi].rearrange("p j (a b t) -> p a j b t", b=2, t=HALVES),
+            )
+
+        def swq(s, lo, hi):
+            nc.scalar.copy(
+                out=w_bf[s][:, :, lo:hi, :].rearrange("p t q j -> p q j t"),
+                in_=w_raw[s][:, :, HALVES * lo : HALVES * hi].rearrange("p j (q t) -> p q j t", t=HALVES),
+            )
+
+        sx(0, 384, N)
         vx(0, 0, 256)
-        vx(0, 256, 344)
+        vx(0, 256, 384)
         quantize_x(0, 0, 256)
+        swq(0, 80, P)
+        vwq(0, 0, 80)
         quantize_x(0, 256, N)
-        sw(0, 0)
-        vw(0, 1)
         quantize_w(0, 0, 1)
         quantize_w(0, 1, 2)
         multiply(0)
-        vx(1, 0, 256)
-        tanh(0, 0)
-        tanh(0, 1)
-        vw_all(1)
-        quantize_x(1, 0, 256)
-        quantize_w(1, 0, 2)
         sx(1, 424, N)
+        vx(1, 0, 256)
         vx(1, 256, 424)
+        quantize_x(1, 0, 256)
+        tanh(0, 0)
+        swq(1, 80, P)
+        vwq(1, 0, 80)
         quantize_x(1, 256, N)
+        quantize_w(1, 0, 1)
+        quantize_w(1, 1, 2)
         multiply(1)
-        tanh(1, 0)
-        tanh(1, 1)
         for g in range(G):
             for t in range(HALVES):
-                if g >= SIDE:
+                if (g, t) != (0, 0):
                     tanh(g, t)
                 add(g, t)
             store(g, nc.sync)

@@ -20,7 +20,8 @@ SIDE = P // ROWS
 PAIRS = G // SIDE
 HALVES = M // P
 RUN = 4
-VECTOR_COLUMNS = 344
+X_VECTOR = 352
+W_VECTOR = 80
 
 
 def tile_rows_glin_tanh_res_kernel(tc, x, w, r, out):
@@ -42,43 +43,20 @@ def tile_rows_glin_tanh_res_kernel(tc, x, w, r, out):
         w_codes = [sbuf.tile([P, M], U32, name="w_codes%d" % s, align_bytes=64) for s in range(PAIRS)]
         w_scales = [sbuf.tile([P, M], U8, name="w_scales%d" % s, align_bytes=64) for s in range(PAIRS)]
         sums = [[psum.tile([P, N], F32, name="sums%d_%d" % (g, t)) for t in range(HALVES)] for g in range(G)]
-        warm_in = sbuf.tile([P, 1], F32, name="warm_in")
-        warm_out = sbuf.tile([P, 1], F32, name="warm_out")
 
-        def load_x(s, lo, hi, eng):
-            eng.dma_start(
-                out=x_raw[s][:, :, lo:hi],
-                in_=x[SIDE * s : SIDE * (s + 1), :, lo:hi].rearrange("c (p j) n -> (c p) j n", j=PACK),
+        def round_x(copy, s, lo, hi):
+            copy(
+                out=x_bf[s][:, lo:hi, :].rearrange("p (a i) j -> p a j i", i=RUN),
+                in_=x_raw[s][:, :, lo:hi].rearrange("p j (a i) -> p a j i", i=RUN),
             )
 
-        def load_w(s, eng):
-            eng.dma_start(
-                out=w_raw[s][:],
-                in_=w[SIDE * s : SIDE * (s + 1)].rearrange("c (p j) m -> (c p) j m", j=PACK),
+        def round_w(copy, s, lo, hi):
+            copy(
+                out=w_bf[s][:, :, lo:hi, :].rearrange("p t (a b) j -> p a j b t", b=RUN // HALVES),
+                in_=w_raw[s][:, :, HALVES * lo : HALVES * hi].rearrange(
+                    "p j (a b t) -> p a j b t", b=RUN // HALVES, t=HALVES
+                ),
             )
-
-        def load_r(g, eng):
-            eng.dma_start(out=res[g][:], in_=r[g].rearrange("(p t) n -> p t n", t=HALVES))
-
-        load_x(0, 0, N, nc.sync)
-        load_w(0, nc.sync)
-        load_x(1, 0, N, nc.sync)
-        load_w(1, nc.sync)
-        for g in range(G):
-            load_r(g, nc.sync)
-
-        nc.vector.memset(warm_in[:], 0.0)
-        nc.scalar.activation(out=warm_out[:], in_=warm_in[:], func=TANH)
-
-        def x_views(s, lo, hi):
-            dst = x_bf[s][:, lo:hi, :].rearrange("p (a i) j -> p a j i", i=RUN)
-            src = x_raw[s][:, :, lo:hi].rearrange("p j (a i) -> p a j i", i=RUN)
-            return dst, src
-
-        def w_views(s, t):
-            dst = w_bf[s][:, t, :, :]
-            src = w_raw[s][:].rearrange("p j (q t) -> p t q j", t=HALVES)[:, t, :, :]
-            return dst, src
 
         def quantize_x(s, lo, hi):
             nc.vector.quantize_mx(
@@ -87,11 +65,11 @@ def tile_rows_glin_tanh_res_kernel(tc, x, w, r, out):
                 in_=x_bf[s][:, lo:hi, :].rearrange("p n j -> p (n j)"),
             )
 
-        def quantize_w(s, lo, hi):
+        def quantize_w(s, t):
             nc.vector.quantize_mx(
-                out=w_codes[s][:, P * lo : P * hi].bitcast(FP8X4),
-                scales=w_scales[s][:, P * lo : P * hi],
-                in_=w_bf[s][:, lo:hi, :, :].rearrange("p t q j -> p (t q j)"),
+                out=w_codes[s][:, P * t : P * (t + 1)].bitcast(FP8X4),
+                scales=w_scales[s][:, P * t : P * (t + 1)],
+                in_=w_bf[s][:, t, :, :].rearrange("p q j -> p (q j)"),
             )
 
         def multiply(s):
@@ -109,70 +87,58 @@ def tile_rows_glin_tanh_res_kernel(tc, x, w, r, out):
                         stop=True,
                     )
 
-        def vx(s, lo, hi):
-            dst, src = x_views(s, lo, hi)
-            nc.vector.tensor_copy(out=dst, in_=src)
-
-        def sx(s, lo, hi):
-            dst, src = x_views(s, lo, hi)
-            nc.scalar.copy(out=dst, in_=src)
-
-        def vw(s, t):
-            dst, src = w_views(s, t)
-            nc.vector.tensor_copy(out=dst, in_=src)
-
-        def sw(s, t):
-            dst, src = w_views(s, t)
-            nc.scalar.copy(out=dst, in_=src)
-
-        def vw_all(s):
-            nc.vector.tensor_copy(out=w_bf[s][:], in_=w_raw[s][:].rearrange("p j (q t) -> p t q j", t=HALVES))
-
         def tanh(g, t):
             nc.scalar.activation(out=act[g][:, t, :], in_=sums[g][t][:], func=TANH)
 
         def add(g, t):
             nc.vector.tensor_tensor(out=act[g][:, t, :], in0=act[g][:, t, :], in1=res[g][:, t, :], op=ADD)
 
-        def store(g, eng):
-            eng.dma_start(out=out[g].rearrange("(p t) n -> p t n", t=HALVES), in_=act[g][:])
-
-        def vwq(s, lo, hi):
-            nc.vector.tensor_copy(
-                out=w_bf[s][:, :, lo:hi, :].rearrange("p t (a b) j -> p a j b t", b=2),
-                in_=w_raw[s][:, :, HALVES * lo : HALVES * hi].rearrange("p j (a b t) -> p a j b t", b=2, t=HALVES),
+        def load_x(s):
+            nc.sync.dma_start(
+                out=x_raw[s][:],
+                in_=x[SIDE * s : SIDE * (s + 1)].rearrange("c (p j) n -> (c p) j n", j=PACK),
             )
 
-        def swq(s, lo, hi):
-            nc.scalar.copy(
-                out=w_bf[s][:, :, lo:hi, :].rearrange("p t q j -> p q j t"),
-                in_=w_raw[s][:, :, HALVES * lo : HALVES * hi].rearrange("p j (q t) -> p q j t", t=HALVES),
+        def load_r(g):
+            nc.sync.dma_start(out=res[g][:], in_=r[g].rearrange("(p t) n -> p t n", t=HALVES))
+
+
+        vector_copy = nc.vector.tensor_copy
+        scalar_copy = nc.scalar.copy
+
+        def load_w(s):
+            nc.sync.dma_start(
+                out=w_raw[s][:],
+                in_=w[SIDE * s : SIDE * (s + 1)].rearrange("c (p j) m -> (c p) j m", j=PACK),
             )
 
-        sx(0, 384, N)
-        vx(0, 0, 256)
-        vx(0, 256, 384)
-        quantize_x(0, 0, 256)
-        swq(0, 80, P)
-        vwq(0, 0, 80)
-        quantize_x(0, 256, N)
-        quantize_w(0, 0, 1)
-        quantize_w(0, 1, 2)
-        multiply(0)
-        sx(1, 424, N)
-        vx(1, 0, 256)
-        vx(1, 256, 424)
-        quantize_x(1, 0, 256)
+        def store_half(g, t):
+            nc.sync.dma_start(out=out[g].rearrange("(p t) n -> p t n", t=HALVES)[:, t, :], in_=act[g][:, t, :])
+
+        def prepare(s):
+            round_x(scalar_copy, s, X_VECTOR, N)
+            round_w(scalar_copy, s, W_VECTOR, P)
+            round_x(vector_copy, s, 0, N // 2)
+            round_x(vector_copy, s, N // 2, X_VECTOR)
+            quantize_x(s, 0, N // 2)
+            round_w(vector_copy, s, 0, W_VECTOR)
+            quantize_x(s, N // 2, N)
+            for t in range(HALVES):
+                quantize_w(s, t)
+            multiply(s)
+
+        for s in range(PAIRS):
+            load_x(s)
+            load_w(s)
+        for g in range(G):
+            load_r(g)
+
+        prepare(0)
         tanh(0, 0)
-        swq(1, 80, P)
-        vwq(1, 0, 80)
-        quantize_x(1, 256, N)
-        quantize_w(1, 0, 1)
-        quantize_w(1, 1, 2)
-        multiply(1)
+        prepare(1)
         for g in range(G):
             for t in range(HALVES):
                 if (g, t) != (0, 0):
                     tanh(g, t)
                 add(g, t)
-            store(g, nc.sync)
+                store_half(g, t)

@@ -32,16 +32,16 @@ def tile_rows_glin_tanh_res_kernel(tc, x, w, r, out):
         psum = ctx.enter_context(tc.psum_pool(name="psum", bufs=1))
         ctx.enter_context(tc.manual_schedule())
 
-        x_raw = [sbuf.tile([P, PACK, N], F32, name="x_raw%d" % s, align_bytes=64) for s in range(PAIRS)]
-        w_raw = [sbuf.tile([P, PACK, M], F32, name="w_raw%d" % s, align_bytes=64) for s in range(PAIRS)]
-        res = [sbuf.tile([P, HALVES, N], F32, name="res%d" % g, align_bytes=64) for g in range(G)]
-        act = [sbuf.tile([P, HALVES, N], F32, name="act%d" % g, align_bytes=64) for g in range(G)]
-        x_bf = [sbuf.tile([P, N, PACK], BF16, name="x_bf%d" % s, align_bytes=64) for s in range(PAIRS)]
-        w_bf = [sbuf.tile([P, HALVES, P, PACK], BF16, name="w_bf%d" % s, align_bytes=64) for s in range(PAIRS)]
-        x_codes = [sbuf.tile([P, N], U32, name="x_codes%d" % s, align_bytes=64) for s in range(PAIRS)]
-        x_scales = [sbuf.tile([P, N], U8, name="x_scales%d" % s, align_bytes=64) for s in range(PAIRS)]
-        w_codes = [sbuf.tile([P, M], U32, name="w_codes%d" % s, align_bytes=64) for s in range(PAIRS)]
-        w_scales = [sbuf.tile([P, M], U8, name="w_scales%d" % s, align_bytes=64) for s in range(PAIRS)]
+        x_raw = [sbuf.tile([P, PACK, N], F32, name="x_raw%d" % s, align_bytes=256) for s in range(PAIRS)]
+        w_raw = [sbuf.tile([P, PACK, M], F32, name="w_raw%d" % s, align_bytes=256) for s in range(PAIRS)]
+        res = [sbuf.tile([P, HALVES, N], F32, name="res%d" % g, align_bytes=256) for g in range(G)]
+        act = [sbuf.tile([P, HALVES, N], F32, name="act%d" % g, align_bytes=256) for g in range(G)]
+        x_bf = [sbuf.tile([P, N, PACK], BF16, name="x_bf%d" % s, align_bytes=256) for s in range(PAIRS)]
+        w_bf = [sbuf.tile([P, HALVES, P, PACK], BF16, name="w_bf%d" % s, align_bytes=256) for s in range(PAIRS)]
+        x_codes = [sbuf.tile([P, N], U32, name="x_codes%d" % s, align_bytes=256) for s in range(PAIRS)]
+        x_scales = [sbuf.tile([P, N], U8, name="x_scales%d" % s, align_bytes=256) for s in range(PAIRS)]
+        w_codes = [sbuf.tile([P, M], U32, name="w_codes%d" % s, align_bytes=256) for s in range(PAIRS)]
+        w_scales = [sbuf.tile([P, M], U8, name="w_scales%d" % s, align_bytes=256) for s in range(PAIRS)]
         sums = [[psum.tile([P, N], F32, name="sums%d_%d" % (g, t)) for t in range(HALVES)] for g in range(G)]
 
         def round_x(copy, s, lo, hi):

@@ -32,10 +32,10 @@ def tile_rows_glin_tanh_res_kernel(tc, x, w, r, out):
         psum = ctx.enter_context(tc.psum_pool(name="psum", bufs=1))
         ctx.enter_context(tc.manual_schedule())
 
-        x_raw = [sbuf.tile([P, PACK, N], F32, name="x_raw%d" % s, align_bytes=256) for s in range(PAIRS)]
-        w_raw = [sbuf.tile([P, PACK, M], F32, name="w_raw%d" % s, align_bytes=256) for s in range(PAIRS)]
-        res = [sbuf.tile([P, HALVES, N], F32, name="res%d" % g, align_bytes=256) for g in range(G)]
-        act = [sbuf.tile([P, HALVES, N], F32, name="act%d" % g, align_bytes=256) for g in range(G)]
+        x_raw = [sbuf.tile([P, PACK, N], F32, name="x_raw%d" % s, align_bytes=4096) for s in range(PAIRS)]
+        w_raw = [sbuf.tile([P, PACK, M], F32, name="w_raw%d" % s, align_bytes=4096) for s in range(PAIRS)]
+        res = [sbuf.tile([P, HALVES, N], F32, name="res%d" % g, align_bytes=4096) for g in range(G)]
+        act = [sbuf.tile([P, HALVES, N], F32, name="act%d" % g, align_bytes=4096) for g in range(G)]
         x_bf = [sbuf.tile([P, N, PACK], BF16, name="x_bf%d" % s, align_bytes=256) for s in range(PAIRS)]
         w_bf = [sbuf.tile([P, HALVES, P, PACK], BF16, name="w_bf%d" % s, align_bytes=256) for s in range(PAIRS)]
         x_codes = [sbuf.tile([P, N], U32, name="x_codes%d" % s, align_bytes=256) for s in range(PAIRS)]

@@ -100,7 +100,8 @@ def tile_rows_glin_tanh_res_kernel(tc, x, w, r, out):
             )
 
         def load_r(g):
-            nc.sync.dma_start(out=res[g][:], in_=r[g].rearrange("(p t) n -> p t n", t=HALVES))
+            for t in range(HALVES):
+                nc.sync.dma_start(out=res[g][:, t, :], in_=r[g].rearrange("(p t) n -> p t n", t=HALVES)[:, t, :])
 
 
         vector_copy = nc.vector.tensor_copy
@@ -112,8 +113,8 @@ def tile_rows_glin_tanh_res_kernel(tc, x, w, r, out):
                 in_=w[SIDE * s : SIDE * (s + 1)].rearrange("c (p j) m -> (c p) j m", j=PACK),
             )
 
-        def store_half(g, t):
-            nc.sync.dma_start(out=out[g].rearrange("(p t) n -> p t n", t=HALVES)[:, t, :], in_=act[g][:, t, :])
+        def store(g):
+            nc.sync.dma_start(out=out[g].rearrange("(p t) n -> p t n", t=HALVES), in_=act[g][:])
 
         def prepare(s):
             round_x(scalar_copy, s, X_VECTOR, N)
@@ -141,4 +142,4 @@ def tile_rows_glin_tanh_res_kernel(tc, x, w, r, out):
                 if (g, t) != (0, 0):
                     tanh(g, t)
                 add(g, t)
-                store_half(g, t)
+            store(g)

@@ -20,8 +20,7 @@ SIDE = P // ROWS
 PAIRS = G // SIDE
 HALVES = M // P
 RUN = 4
-X_VECTOR = 352
-W_VECTOR = 80
+X_VECTOR = 288
 
 
 def tile_rows_glin_tanh_res_kernel(tc, x, w, r, out):
@@ -32,17 +31,26 @@ def tile_rows_glin_tanh_res_kernel(tc, x, w, r, out):
         psum = ctx.enter_context(tc.psum_pool(name="psum", bufs=1))
         ctx.enter_context(tc.manual_schedule())
 
-        x_raw = [sbuf.tile([P, PACK, N], F32, name="x_raw%d" % s, align_bytes=4096) for s in range(PAIRS)]
-        w_raw = [sbuf.tile([P, PACK, M], F32, name="w_raw%d" % s, align_bytes=4096) for s in range(PAIRS)]
-        res = [sbuf.tile([P, HALVES, N], F32, name="res%d" % g, align_bytes=4096) for g in range(G)]
-        act = [sbuf.tile([P, HALVES, N], F32, name="act%d" % g, align_bytes=4096) for g in range(G)]
-        x_bf = [sbuf.tile([P, N, PACK], BF16, name="x_bf%d" % s, align_bytes=256) for s in range(PAIRS)]
-        w_bf = [sbuf.tile([P, HALVES, P, PACK], BF16, name="w_bf%d" % s, align_bytes=256) for s in range(PAIRS)]
-        x_codes = [sbuf.tile([P, N], U32, name="x_codes%d" % s, align_bytes=256) for s in range(PAIRS)]
-        x_scales = [sbuf.tile([P, N], U8, name="x_scales%d" % s, align_bytes=256) for s in range(PAIRS)]
-        w_codes = [sbuf.tile([P, M], U32, name="w_codes%d" % s, align_bytes=256) for s in range(PAIRS)]
-        w_scales = [sbuf.tile([P, M], U8, name="w_scales%d" % s, align_bytes=256) for s in range(PAIRS)]
+        def tiles(name, count, shape, dtype, align):
+            return [sbuf.tile(shape, dtype, name="%s%d" % (name, i), align_bytes=align) for i in range(count)]
+
+        x_raw = tiles("x_raw", PAIRS, [P, PACK, N], F32, 4096)
+        w_raw = tiles("w_raw", PAIRS, [P, PACK, M], F32, 4096)
+        res = tiles("res", G, [P, HALVES, N], F32, 4096)
+        act = tiles("act", G, [P, HALVES, N], F32, 4096)
+        x_bf = tiles("x_bf", PAIRS, [P, N, PACK], BF16, 256)
+        w_bf = tiles("w_bf", PAIRS, [P, HALVES, P, PACK], BF16, 256)
+        x_codes = tiles("x_codes", PAIRS, [P, N], U32, 256)
+        x_scales = tiles("x_scales", PAIRS, [P, N], U8, 256)
+        w_codes = tiles("w_codes", PAIRS, [P, M], U32, 256)
+        w_scales = tiles("w_scales", PAIRS, [P, M], U8, 256)
         sums = [[psum.tile([P, N], F32, name="sums%d_%d" % (g, t)) for t in range(HALVES)] for g in range(G)]
+
+        def load_operand(tile, dram, s):
+            nc.sync.dma_start(
+                out=tile[s][:],
+                in_=dram[SIDE * s : SIDE * (s + 1)].rearrange("c (p j) n -> (c p) j n", j=PACK),
+            )
 
         def round_x(copy, s, lo, hi):
             copy(
@@ -50,26 +58,24 @@ def tile_rows_glin_tanh_res_kernel(tc, x, w, r, out):
                 in_=x_raw[s][:, :, lo:hi].rearrange("p j (a i) -> p a j i", i=RUN),
             )
 
-        def round_w(copy, s, lo, hi):
+        def round_w(copy, s):
             copy(
-                out=w_bf[s][:, :, lo:hi, :].rearrange("p t (a b) j -> p a j b t", b=RUN // HALVES),
-                in_=w_raw[s][:, :, HALVES * lo : HALVES * hi].rearrange(
-                    "p j (a b t) -> p a j b t", b=RUN // HALVES, t=HALVES
-                ),
+                out=w_bf[s][:].rearrange("p t (a b) j -> p a j b t", b=RUN // HALVES),
+                in_=w_raw[s][:].rearrange("p j (a b t) -> p a j b t", b=RUN // HALVES, t=HALVES),
             )
 
-        def quantize_x(s, lo, hi):
+        def quantize_x(s):
             nc.vector.quantize_mx(
-                out=x_codes[s][:, lo:hi].bitcast(FP8X4),
-                scales=x_scales[s][:, lo:hi],
-                in_=x_bf[s][:, lo:hi, :].rearrange("p n j -> p (n j)"),
+                out=x_codes[s][:].bitcast(FP8X4),
+                scales=x_scales[s][:],
+                in_=x_bf[s][:].rearrange("p n j -> p (n j)"),
             )
 
-        def quantize_w(s, t):
+        def quantize_w(s):
             nc.vector.quantize_mx(
-                out=w_codes[s][:, P * t : P * (t + 1)].bitcast(FP8X4),
-                scales=w_scales[s][:, P * t : P * (t + 1)],
-                in_=w_bf[s][:, t, :, :].rearrange("p q j -> p (q j)"),
+                out=w_codes[s][:].bitcast(FP8X4),
+                scales=w_scales[s][:],
+                in_=w_bf[s][:].rearrange("p t q j -> p (t q j)"),
             )
 
         def multiply(s):
@@ -93,53 +99,27 @@ def tile_rows_glin_tanh_res_kernel(tc, x, w, r, out):
         def add(g, t):
             nc.vector.tensor_tensor(out=act[g][:, t, :], in0=act[g][:, t, :], in1=res[g][:, t, :], op=ADD)
 
-        def load_x(s):
-            nc.sync.dma_start(
-                out=x_raw[s][:],
-                in_=x[SIDE * s : SIDE * (s + 1)].rearrange("c (p j) n -> (c p) j n", j=PACK),
-            )
-
-        def load_r(g):
-            for t in range(HALVES):
-                nc.sync.dma_start(out=res[g][:, t, :], in_=r[g].rearrange("(p t) n -> p t n", t=HALVES)[:, t, :])
-
-
-        vector_copy = nc.vector.tensor_copy
-        scalar_copy = nc.scalar.copy
-
-        def load_w(s):
-            nc.sync.dma_start(
-                out=w_raw[s][:],
-                in_=w[SIDE * s : SIDE * (s + 1)].rearrange("c (p j) m -> (c p) j m", j=PACK),
-            )
-
-        def store(g):
-            nc.sync.dma_start(out=out[g].rearrange("(p t) n -> p t n", t=HALVES), in_=act[g][:])
+        def dealt(dram, g):
+            return dram[g].rearrange("(p t) n -> p t n", t=HALVES)
 
         def prepare(s):
-            round_x(scalar_copy, s, X_VECTOR, N)
-            round_w(scalar_copy, s, W_VECTOR, P)
-            round_x(vector_copy, s, 0, N // 2)
-            round_x(vector_copy, s, N // 2, X_VECTOR)
-            quantize_x(s, 0, N // 2)
-            round_w(vector_copy, s, 0, W_VECTOR)
-            quantize_x(s, N // 2, N)
-            for t in range(HALVES):
-                quantize_w(s, t)
+            round_x(nc.scalar.copy, s, X_VECTOR, N)
+            round_x(nc.vector.tensor_copy, s, 0, X_VECTOR)
+            round_w(nc.vector.tensor_copy, s)
+            quantize_x(s)
+            quantize_w(s)
             multiply(s)
 
         for s in range(PAIRS):
-            load_x(s)
-            load_w(s)
+            load_operand(x_raw, x, s)
+            load_operand(w_raw, w, s)
         for g in range(G):
-            load_r(g)
+            nc.sync.dma_start(out=res[g][:], in_=dealt(r, g))
 
-        prepare(0)
-        tanh(0, 0)
-        prepare(1)
+        for s in range(PAIRS):
+            prepare(s)
         for g in range(G):
             for t in range(HALVES):
-                if (g, t) != (0, 0):
-                    tanh(g, t)
+                tanh(g, t)
                 add(g, t)
-            store(g)
+                nc.sync.dma_start(out=dealt(out, g)[:, t, :], in_=act[g][:, t, :])

@@ -21,6 +21,7 @@ PAIRS = G // SIDE
 HALVES = M // P
 RUN = 4
 X_VECTOR = 288
+R_CUTS = ((0, 2), (2, 5), (5, 8))
 
 
 def tile_rows_glin_tanh_res_kernel(tc, x, w, r, out):
@@ -36,7 +37,7 @@ def tile_rows_glin_tanh_res_kernel(tc, x, w, r, out):
 
         x_raw = tiles("x_raw", PAIRS, [P, PACK, N], F32, 4096)
         w_raw = tiles("w_raw", PAIRS, [P, PACK, M], F32, 4096)
-        res = tiles("res", G, [P, HALVES, N], F32, 4096)
+        res = [sbuf.tile([P, hi - lo, N], F32, name="res%d" % lo, align_bytes=4096) for lo, hi in R_CUTS]
         act = tiles("act", G, [P, HALVES, N], F32, 4096)
         x_bf = tiles("x_bf", PAIRS, [P, N, PACK], BF16, 256)
         w_bf = tiles("w_bf", PAIRS, [P, HALVES, P, PACK], BF16, 256)
@@ -60,8 +61,8 @@ def tile_rows_glin_tanh_res_kernel(tc, x, w, r, out):
 
         def round_w(copy, s):
             copy(
-                out=w_bf[s][:].rearrange("p t (a b) j -> p a j b t", b=RUN // HALVES),
-                in_=w_raw[s][:].rearrange("p j (a b t) -> p a j b t", b=RUN // HALVES, t=HALVES),
+                out=w_bf[s][:].rearrange("p t (a i) j -> p (t a) j i", i=RUN),
+                in_=w_raw[s][:].rearrange("p j (a i) -> p a j i", i=RUN),
             )
 
         def quantize_x(s):
@@ -97,24 +98,37 @@ def tile_rows_glin_tanh_res_kernel(tc, x, w, r, out):
             nc.scalar.activation(out=act[g][:, t, :], in_=sums[g][t][:], func=TANH)
 
         def add(g, t):
-            nc.vector.tensor_tensor(out=act[g][:, t, :], in0=act[g][:, t, :], in1=res[g][:, t, :], op=ADD)
+            u = HALVES * g + t
+            piece = [k for k, (lo, hi) in enumerate(R_CUTS) if lo <= u < hi][0]
+            nc.vector.tensor_tensor(
+                out=act[g][:, t, :], in0=act[g][:, t, :], in1=res[piece][:, u - R_CUTS[piece][0], :], op=ADD
+            )
 
-        def dealt(dram, g):
-            return dram[g].rearrange("(p t) n -> p t n", t=HALVES)
+        def blocks(dram):
+            return dram.rearrange("g (t p) n -> p (g t) n", t=HALVES)
 
         def prepare(s):
             round_x(nc.scalar.copy, s, X_VECTOR, N)
-            round_x(nc.vector.tensor_copy, s, 0, X_VECTOR)
-            round_w(nc.vector.tensor_copy, s)
-            quantize_x(s)
-            quantize_w(s)
+            if s == 0:
+                round_w(nc.vector.tensor_copy, s)
+                quantize_w(s)
+                round_x(nc.vector.tensor_copy, s, 0, X_VECTOR)
+                quantize_x(s)
+            else:
+                round_x(nc.vector.tensor_copy, s, 0, X_VECTOR)
+                round_w(nc.vector.tensor_copy, s)
+                quantize_x(s)
+                quantize_w(s)
             multiply(s)
 
-        for s in range(PAIRS):
-            load_operand(x_raw, x, s)
-            load_operand(w_raw, w, s)
-        for g in range(G):
-            nc.sync.dma_start(out=res[g][:], in_=dealt(r, g))
+        rows = w[0:SIDE].rearrange("c (p e j) n -> e (c p) j n", e=2, j=PACK)
+        for e in range(2):
+            nc.sync.dma_start(out=w_raw[0][e:P:2], in_=rows[e])
+        load_operand(x_raw, x, 0)
+        load_operand(x_raw, x, 1)
+        load_operand(w_raw, w, 1)
+        for k, (lo, hi) in enumerate(R_CUTS):
+            nc.sync.dma_start(out=res[k][:], in_=blocks(r)[:, lo:hi, :])
 
         for s in range(PAIRS):
             prepare(s)
@@ -122,4 +136,4 @@ def tile_rows_glin_tanh_res_kernel(tc, x, w, r, out):
             for t in range(HALVES):
                 tanh(g, t)
                 add(g, t)
-                nc.sync.dma_start(out=dealt(out, g)[:, t, :], in_=act[g][:, t, :])
+                nc.sync.dma_start(out=blocks(out)[:, HALVES * g + t, :], in_=act[g][:, t, :])

@@ -20,8 +20,8 @@ SIDE = P // ROWS
 PAIRS = G // SIDE
 HALVES = M // P
 RUN = 4
-X_VECTOR = 288
-R_CUTS = ((0, 2), (2, 5), (5, 8))
+X_HALF = N // 2
+X_VECTOR = 320
 
 
 def tile_rows_glin_tanh_res_kernel(tc, x, w, r, out):
@@ -36,8 +36,9 @@ def tile_rows_glin_tanh_res_kernel(tc, x, w, r, out):
             return [sbuf.tile(shape, dtype, name="%s%d" % (name, i), align_bytes=align) for i in range(count)]
 
         x_raw = tiles("x_raw", PAIRS, [P, PACK, N], F32, 4096)
-        w_raw = tiles("w_raw", PAIRS, [P, PACK, M], F32, 4096)
-        res = [sbuf.tile([P, hi - lo, N], F32, name="res%d" % lo, align_bytes=4096) for lo, hi in R_CUTS]
+        w_both = sbuf.tile([P, PAIRS, PACK, M], F32, name="w_both", align_bytes=4096)
+        w_raw = [w_both[:, s] for s in range(PAIRS)]
+        res = tiles("res", G, [P, HALVES, N], F32, 4096)
         act = tiles("act", G, [P, HALVES, N], F32, 4096)
         x_bf = tiles("x_bf", PAIRS, [P, N, PACK], BF16, 256)
         w_bf = tiles("w_bf", PAIRS, [P, HALVES, P, PACK], BF16, 256)
@@ -61,15 +62,15 @@ def tile_rows_glin_tanh_res_kernel(tc, x, w, r, out):
 
         def round_w(copy, s):
             copy(
-                out=w_bf[s][:].rearrange("p t (a i) j -> p (t a) j i", i=RUN),
-                in_=w_raw[s][:].rearrange("p j (a i) -> p a j i", i=RUN),
+                out=w_bf[s][:].rearrange("p t (a b) j -> p a j b t", b=RUN // HALVES),
+                in_=w_raw[s].rearrange("p j (a b t) -> p a j b t", b=RUN // HALVES, t=HALVES),
             )
 
-        def quantize_x(s):
+        def quantize_x(s, lo, hi):
             nc.vector.quantize_mx(
-                out=x_codes[s][:].bitcast(FP8X4),
-                scales=x_scales[s][:],
-                in_=x_bf[s][:].rearrange("p n j -> p (n j)"),
+                out=x_codes[s][:, lo:hi].bitcast(FP8X4),
+                scales=x_scales[s][:, lo:hi],
+                in_=x_bf[s][:, lo:hi, :].rearrange("p n j -> p (n j)"),
             )
 
         def quantize_w(s):
@@ -98,42 +99,42 @@ def tile_rows_glin_tanh_res_kernel(tc, x, w, r, out):
             nc.scalar.activation(out=act[g][:, t, :], in_=sums[g][t][:], func=TANH)
 
         def add(g, t):
-            u = HALVES * g + t
-            piece = [k for k, (lo, hi) in enumerate(R_CUTS) if lo <= u < hi][0]
-            nc.vector.tensor_tensor(
-                out=act[g][:, t, :], in0=act[g][:, t, :], in1=res[piece][:, u - R_CUTS[piece][0], :], op=ADD
-            )
+            nc.vector.tensor_tensor(out=act[g][:, t, :], in0=act[g][:, t, :], in1=res[g][:, t, :], op=ADD)
 
-        def blocks(dram):
-            return dram.rearrange("g (t p) n -> p (g t) n", t=HALVES)
+        def dealt(dram, g):
+            return dram[g].rearrange("(p t) n -> p t n", t=HALVES)
 
-        def prepare(s):
-            round_x(nc.scalar.copy, s, X_VECTOR, N)
-            if s == 0:
-                round_w(nc.vector.tensor_copy, s)
-                quantize_w(s)
-                round_x(nc.vector.tensor_copy, s, 0, X_VECTOR)
-                quantize_x(s)
-            else:
-                round_x(nc.vector.tensor_copy, s, 0, X_VECTOR)
-                round_w(nc.vector.tensor_copy, s)
-                quantize_x(s)
-                quantize_w(s)
-            multiply(s)
+        def finish(g, t):
+            add(g, t)
+            nc.sync.dma_start(out=dealt(out, g)[:, t, :], in_=act[g][:, t, :])
 
-        rows = w[0:SIDE].rearrange("c (p e j) n -> e (c p) j n", e=2, j=PACK)
+        rows = x[0:SIDE].rearrange("c (p e j) n -> e (c p) j n", e=2, j=PACK)
         for e in range(2):
-            nc.sync.dma_start(out=w_raw[0][e:P:2], in_=rows[e])
-        load_operand(x_raw, x, 0)
+            nc.sync.dma_start(out=x_raw[0][e:P:2], in_=rows[e])
+        nc.sync.dma_start(
+            out=w_both[:].rearrange("p s j m -> p s (j m)"),
+            in_=w.rearrange("(s c) (p j) m -> (c p) s (j m)", c=SIDE, j=PACK),
+        )
         load_operand(x_raw, x, 1)
-        load_operand(w_raw, w, 1)
-        for k, (lo, hi) in enumerate(R_CUTS):
-            nc.sync.dma_start(out=res[k][:], in_=blocks(r)[:, lo:hi, :])
+        for g in range(G):
+            nc.sync.dma_start(out=res[g][:], in_=dealt(r, g))
 
-        for s in range(PAIRS):
-            prepare(s)
+        round_x(nc.vector.tensor_copy, 0, 0, X_HALF)
+        round_x(nc.vector.tensor_copy, 0, X_HALF, N)
+        quantize_x(0, 0, X_HALF)
+        quantize_x(0, X_HALF, N)
+        round_w(nc.vector.tensor_copy, 0)
+        round_w(nc.scalar.copy, 1)
+        quantize_w(0)
+        multiply(0)
+        quantize_w(1)
+        round_x(nc.scalar.copy, 1, X_VECTOR, N)
+        round_x(nc.vector.tensor_copy, 1, 0, X_HALF)
+        round_x(nc.vector.tensor_copy, 1, X_HALF, X_VECTOR)
+        quantize_x(1, 0, X_HALF)
+        quantize_x(1, X_HALF, N)
+        multiply(1)
         for g in range(G):
             for t in range(HALVES):
                 tanh(g, t)
-                add(g, t)
-                nc.sync.dma_start(out=blocks(out)[:, HALVES * g + t, :], in_=act[g][:, t, :])
+                finish(g, t)

@@ -109,8 +109,8 @@ def tile_rows_glin_tanh_res_kernel(tc, x, w, r, out):
             nc.sync.dma_start(out=dealt(out, g)[:, t, :], in_=act[g][:, t, :])
 
         rows = x[0:SIDE].rearrange("c (p e j) n -> e (c p) j n", e=2, j=PACK)
-        for e in range(2):
-            nc.sync.dma_start(out=x_raw[0][e:P:2], in_=rows[e])
+        for e, queue in enumerate((nc.sync, nc.scalar)):
+            queue.dma_start(out=x_raw[0][e:P:2], in_=rows[e])
         nc.sync.dma_start(
             out=w_both[:].rearrange("p s j m -> p s (j m)"),
             in_=w.rearrange("(s c) (p j) m -> (c p) s (j m)", c=SIDE, j=PACK),

@@ -20,8 +20,11 @@ SIDE = P // ROWS
 PAIRS = G // SIDE
 HALVES = M // P
 RUN = 4
+DMA_ALIGN = 4096
+MX_ALIGN = 256
 X_HALF = N // 2
 X_VECTOR = 320
+W_VECTOR = 64
 
 
 def tile_rows_glin_tanh_res_kernel(tc, x, w, r, out):
@@ -35,21 +38,20 @@ def tile_rows_glin_tanh_res_kernel(tc, x, w, r, out):
         def tiles(name, count, shape, dtype, align):
             return [sbuf.tile(shape, dtype, name="%s%d" % (name, i), align_bytes=align) for i in range(count)]
 
-        x_raw = tiles("x_raw", PAIRS, [P, PACK, N], F32, 4096)
-        w_both = sbuf.tile([P, PAIRS, PACK, M], F32, name="w_both", align_bytes=4096)
-        w_raw = [w_both[:, s] for s in range(PAIRS)]
-        res = tiles("res", G, [P, HALVES, N], F32, 4096)
-        act = tiles("act", G, [P, HALVES, N], F32, 4096)
-        x_bf = tiles("x_bf", PAIRS, [P, N, PACK], BF16, 256)
-        w_bf = tiles("w_bf", PAIRS, [P, HALVES, P, PACK], BF16, 256)
-        x_codes = tiles("x_codes", PAIRS, [P, N], U32, 256)
-        x_scales = tiles("x_scales", PAIRS, [P, N], U8, 256)
-        w_codes = tiles("w_codes", PAIRS, [P, M], U32, 256)
-        w_scales = tiles("w_scales", PAIRS, [P, M], U8, 256)
+        x_raw = tiles("x_raw", PAIRS, [P, PACK, N], F32, DMA_ALIGN)
+        w_raw = tiles("w_raw", PAIRS, [P, PACK, M], F32, DMA_ALIGN)
+        res = tiles("res", G, [P, HALVES, N], F32, DMA_ALIGN)
+        act = tiles("act", G, [P, HALVES, N], F32, DMA_ALIGN)
+        x_bf = tiles("x_bf", PAIRS, [P, N, PACK], BF16, MX_ALIGN)
+        w_bf = tiles("w_bf", PAIRS, [P, HALVES, P, PACK], BF16, MX_ALIGN)
+        x_codes = tiles("x_codes", PAIRS, [P, N], U32, MX_ALIGN)
+        x_scales = tiles("x_scales", PAIRS, [P, N], U8, MX_ALIGN)
+        w_codes = tiles("w_codes", PAIRS, [P, M], U32, MX_ALIGN)
+        w_scales = tiles("w_scales", PAIRS, [P, M], U8, MX_ALIGN)
         sums = [[psum.tile([P, N], F32, name="sums%d_%d" % (g, t)) for t in range(HALVES)] for g in range(G)]
 
-        def load_operand(tile, dram, s):
-            nc.sync.dma_start(
+        def load_operand(queue, tile, dram, s):
+            queue.dma_start(
                 out=tile[s][:],
                 in_=dram[SIDE * s : SIDE * (s + 1)].rearrange("c (p j) n -> (c p) j n", j=PACK),
             )
@@ -60,10 +62,11 @@ def tile_rows_glin_tanh_res_kernel(tc, x, w, r, out):
                 in_=x_raw[s][:, :, lo:hi].rearrange("p j (a i) -> p a j i", i=RUN),
             )
 
-        def round_w(copy, s):
+        def round_w(copy, s, lo, hi):
+            run = RUN // HALVES
             copy(
-                out=w_bf[s][:].rearrange("p t (a b) j -> p a j b t", b=RUN // HALVES),
-                in_=w_raw[s].rearrange("p j (a b t) -> p a j b t", b=RUN // HALVES, t=HALVES),
+                out=w_bf[s][:, :, lo:hi, :].rearrange("p t (a b) j -> p a j b t", b=run),
+                in_=w_raw[s][:, :, HALVES * lo : HALVES * hi].rearrange("p j (a b t) -> p a j b t", b=run, t=HALVES),
             )
 
         def quantize_x(s, lo, hi):
@@ -104,35 +107,35 @@ def tile_rows_glin_tanh_res_kernel(tc, x, w, r, out):
         def dealt(dram, g):
             return dram[g].rearrange("(p t) n -> p t n", t=HALVES)
 
+        def load_res(g):
+            nc.sync.dma_start(out=res[g][:], in_=dealt(r, g))
+
         def finish(g, t):
             add(g, t)
             nc.sync.dma_start(out=dealt(out, g)[:, t, :], in_=act[g][:, t, :])
 
-        rows = x[0:SIDE].rearrange("c (p e j) n -> e (c p) j n", e=2, j=PACK)
-        for e, queue in enumerate((nc.sync, nc.scalar)):
-            queue.dma_start(out=x_raw[0][e:P:2], in_=rows[e])
-        nc.sync.dma_start(
-            out=w_both[:].rearrange("p s j m -> p s (j m)"),
-            in_=w.rearrange("(s c) (p j) m -> (c p) s (j m)", c=SIDE, j=PACK),
-        )
-        load_operand(x_raw, x, 1)
+        load_operand(nc.sync, x_raw, x, 0)
+        load_operand(nc.scalar, w_raw, w, 0)
+        load_operand(nc.sync, x_raw, x, 1)
+        load_operand(nc.sync, w_raw, w, 1)
         for g in range(G):
-            nc.sync.dma_start(out=res[g][:], in_=dealt(r, g))
+            load_res(g)
 
-        round_x(nc.vector.tensor_copy, 0, 0, X_HALF)
-        round_x(nc.vector.tensor_copy, 0, X_HALF, N)
-        quantize_x(0, 0, X_HALF)
-        quantize_x(0, X_HALF, N)
-        round_w(nc.vector.tensor_copy, 0)
-        round_w(nc.scalar.copy, 1)
+        def prepare_x(s):
+            round_x(nc.scalar.copy, s, X_VECTOR, N)
+            round_x(nc.vector.tensor_copy, s, 0, X_HALF)
+            round_x(nc.vector.tensor_copy, s, X_HALF, X_VECTOR)
+            quantize_x(s, 0, X_HALF)
+            quantize_x(s, X_HALF, N)
+
+        round_w(nc.vector.tensor_copy, 0, 0, P)
         quantize_w(0)
+        prepare_x(0)
         multiply(0)
+        prepare_x(1)
+        round_w(nc.scalar.copy, 1, W_VECTOR, P)
+        round_w(nc.vector.tensor_copy, 1, 0, W_VECTOR)
         quantize_w(1)
-        round_x(nc.scalar.copy, 1, X_VECTOR, N)
-        round_x(nc.vector.tensor_copy, 1, 0, X_HALF)
-        round_x(nc.vector.tensor_copy, 1, X_HALF, X_VECTOR)
-        quantize_x(1, 0, X_HALF)
-        quantize_x(1, X_HALF, N)
         multiply(1)
         for g in range(G):
             for t in range(HALVES):

from contextlib import ExitStack

import concourse.mybir as mybir

G, D, M, N = 4, 256, 256, 512
FLOPS = 2 * G * D * M * N

F32 = mybir.dt.float32
BF16 = mybir.dt.bfloat16
U32 = mybir.dt.uint32
U8 = mybir.dt.uint8
FP8X4 = mybir.dt.float8_e4m3fn_x4
TANH = mybir.ActivationFunctionType.Tanh
ADD = mybir.AluOpType.add

P = 128
PACK = 4
ROWS = D // PACK
SIDE = P // ROWS
PAIRS = G // SIDE
HALVES = M // P
RUN = 4
DMA_ALIGN = 4096
MX_ALIGN = 256
X_HALF = N // 2
X_VECTOR = 320
W_VECTOR = 64


def tile_rows_glin_tanh_res_kernel(tc, x, w, r, out):
    nc = tc.nc

    with ExitStack() as ctx:
        sbuf = ctx.enter_context(tc.tile_pool(name="sbuf", bufs=1))
        psum = ctx.enter_context(tc.psum_pool(name="psum", bufs=1))
        ctx.enter_context(tc.manual_schedule())

        def tiles(name, count, shape, dtype, align):
            return [sbuf.tile(shape, dtype, name="%s%d" % (name, i), align_bytes=align) for i in range(count)]

        x_raw = tiles("x_raw", PAIRS, [P, PACK, N], F32, DMA_ALIGN)
        w_raw = tiles("w_raw", PAIRS, [P, PACK, M], F32, DMA_ALIGN)
        res = tiles("res", G, [P, HALVES, N], F32, DMA_ALIGN)
        act = tiles("act", G, [P, HALVES, N], F32, DMA_ALIGN)
        x_bf = tiles("x_bf", PAIRS, [P, N, PACK], BF16, MX_ALIGN)
        w_bf = tiles("w_bf", PAIRS, [P, HALVES, P, PACK], BF16, MX_ALIGN)
        x_codes = tiles("x_codes", PAIRS, [P, N], U32, MX_ALIGN)
        x_scales = tiles("x_scales", PAIRS, [P, N], U8, MX_ALIGN)
        w_codes = tiles("w_codes", PAIRS, [P, M], U32, MX_ALIGN)
        w_scales = tiles("w_scales", PAIRS, [P, M], U8, MX_ALIGN)
        sums = [[psum.tile([P, N], F32, name="sums%d_%d" % (g, t)) for t in range(HALVES)] for g in range(G)]

        def load_operand(queue, tile, dram, s):
            queue.dma_start(
                out=tile[s][:],
                in_=dram[SIDE * s : SIDE * (s + 1)].rearrange("c (p j) n -> (c p) j n", j=PACK),
            )

        def round_x(copy, s, lo, hi):
            copy(
                out=x_bf[s][:, lo:hi, :].rearrange("p (a i) j -> p a j i", i=RUN),
                in_=x_raw[s][:, :, lo:hi].rearrange("p j (a i) -> p a j i", i=RUN),
            )

        def round_w(copy, s, lo, hi):
            run = RUN // HALVES
            copy(
                out=w_bf[s][:, :, lo:hi, :].rearrange("p t (a b) j -> p a j b t", b=run),
                in_=w_raw[s][:, :, HALVES * lo : HALVES * hi].rearrange("p j (a b t) -> p a j b t", b=run, t=HALVES),
            )

        def quantize_x(s, lo, hi):
            nc.vector.quantize_mx(
                out=x_codes[s][:, lo:hi].bitcast(FP8X4),
                scales=x_scales[s][:, lo:hi],
                in_=x_bf[s][:, lo:hi, :].rearrange("p n j -> p (n j)"),
            )

        def quantize_w(s):
            nc.vector.quantize_mx(
                out=w_codes[s][:].bitcast(FP8X4),
                scales=w_scales[s][:],
                in_=w_bf[s][:].rearrange("p t q j -> p (t q j)"),
            )

        def multiply(s):
            for c in range(SIDE):
                rows = slice(ROWS * c, ROWS * (c + 1))
                for t in range(HALVES):
                    cols = slice(P * t, P * (t + 1))
                    nc.tensor.matmul_mx(
                        out=sums[SIDE * s + c][t][:],
                        lhsT=w_codes[s][rows, cols].bitcast(FP8X4),
                        lhsT_scale=w_scales[s][rows, cols],
                        rhs=x_codes[s][rows, :].bitcast(FP8X4),
                        rhs_scale=x_scales[s][rows, :],
                        start=True,
                        stop=True,
                    )

        def tanh(g, t):
            nc.scalar.activation(out=act[g][:, t, :], in_=sums[g][t][:], func=TANH)

        def add(g, t):
            nc.vector.tensor_tensor(out=act[g][:, t, :], in0=act[g][:, t, :], in1=res[g][:, t, :], op=ADD)

        def dealt(dram, g):
            return dram[g].rearrange("(p t) n -> p t n", t=HALVES)

        def load_res(g):
            nc.sync.dma_start(out=res[g][:], in_=dealt(r, g))

        def finish(g, t):
            add(g, t)
            nc.sync.dma_start(out=dealt(out, g)[:, t, :], in_=act[g][:, t, :])

        load_operand(nc.sync, x_raw, x, 0)
        load_operand(nc.scalar, w_raw, w, 0)
        load_operand(nc.sync, x_raw, x, 1)
        load_operand(nc.sync, w_raw, w, 1)
        for g in range(G):
            load_res(g)

        def prepare_x(s):
            round_x(nc.scalar.copy, s, X_VECTOR, N)
            round_x(nc.vector.tensor_copy, s, 0, X_HALF)
            round_x(nc.vector.tensor_copy, s, X_HALF, X_VECTOR)
            quantize_x(s, 0, X_HALF)
            quantize_x(s, X_HALF, N)

        round_w(nc.vector.tensor_copy, 0, 0, P)
        quantize_w(0)
        prepare_x(0)
        multiply(0)
        prepare_x(1)
        round_w(nc.scalar.copy, 1, W_VECTOR, P)
        round_w(nc.vector.tensor_copy, 1, 0, W_VECTOR)
        quantize_w(1)
        multiply(1)
        for g in range(G):
            for t in range(HALVES):
                tanh(g, t)
                finish(g, t)
